import numpy as np
import ml_dtypes


def mxq(x, axis, fmt="e4m3"):
    dtype, down = {"e4m3": (ml_dtypes.float8_e4m3fn, 7), "e5m2": (ml_dtypes.float8_e5m2, 14)}[fmt]
    v = np.moveaxis(np.asarray(x, np.float32).astype(ml_dtypes.bfloat16).astype(np.float64), axis, -1)
    blocks = v.reshape(v.shape[:-1] + (-1, 32))
    amax = np.abs(blocks).max(-1, keepdims=True)
    byte = np.maximum(np.where(amax > 0, np.frexp(amax)[1] - 1 + 127, 0) - down, 1)
    scale = np.exp2(byte - 127.0)
    codes = (blocks / scale).astype(np.float32).astype(dtype).astype(np.float64)
    return np.moveaxis((codes * scale).reshape(v.shape), -1, axis)


WIDE = False


def mx_kscale(k):
    if not WIDE:
        return np.ones(k)
    levels = np.array([10, -10, 5, -5, 0])
    if k % 512:
        return np.exp2(np.random.permutation(np.resize(levels, k // 32))).repeat(32)
    a = np.empty((k // 512, 16))
    for p in range(k // 512):
        a[p, :8] = np.random.permutation(np.resize(levels, 8))
        for g in range(8):
            far = levels[np.abs(levels - a[p, g]) >= 10]
            a[p, g + 8] = far[np.random.randint(len(far))]
    return np.exp2(a.ravel()).repeat(32)


def f64(x):
    return np.asarray(x).astype(np.float64)


def striped(idx):
    return np.tile(idx.reshape(-1, 16).T, (8, 1)).astype(np.uint16)


def unstriped(offs):
    return offs[:16].T.reshape(-1).astype(np.int64)


def striped8(idx):
    return np.concatenate([x.reshape(-1, 16).T for x in idx]).astype(np.uint16)


def runs(offs, k):
    lists = np.stack([offs[16 * r : 16 * r + 16].T.reshape(-1) for r in range(8)]).astype(np.int64)
    return lists[np.arange(k) % 512 // 64]


def pack_weight(w):
    k, n = w.shape
    w = f64(np.asarray(w, np.float32).astype(ml_dtypes.bfloat16)).reshape(k // 32, 32, n)
    amax = np.abs(w).max(1)
    byte = np.clip(np.where(amax > 0, np.frexp(amax)[1] - 1 + 127 - 7, 1), 1, 254)
    scaled = (w * np.exp2(127.0 - byte)[:, None, :]).reshape(k, n).astype(np.float32)
    words = np.ascontiguousarray(scaled.reshape(k // 512, 128, 4, n).transpose(0, 1, 3, 2)).astype(ml_dtypes.float8_e4m3fn).view(np.uint8)
    return words, np.ascontiguousarray(byte.astype(np.uint8).reshape(k // 512, 16, n))


def unpack_weight(words, scales):
    g, p, n, _ = words.shape
    vals = np.ascontiguousarray(words).view(ml_dtypes.float8_e4m3fn).astype(np.float64) * np.repeat(np.exp2(scales.astype(np.float64) - 127.0), 8, axis=1)[..., None]
    return vals.transpose(0, 1, 3, 2).reshape(g * 512, n)


K, T, S, N, H, W, J, C = 512, 2048, 256, 512, 512, 192, 512, 512


def setup_inputs():
    n = np.random.standard_normal
    s = mx_kscale(K)[:, None]
    u = mx_kscale(K)
    packed_xT = pack_weight(n((K, T)) * s)
    return {
        "x_words": packed_xT[0],
        "x_scales": packed_xT[1],
        "w1": (n((K, H)) / np.sqrt(K) / s).astype(np.float32),
        "gn": (np.random.uniform(0.5, 1.5, (H, 1)) * u[:, None]).astype(np.float32),
        "w2": (n((H, N)) / np.sqrt(H) / u[:, None]).astype(np.float32),
        "gs": (np.random.uniform(0.5, 1.5, (K, 1)) / s).astype(np.float32),
        "offs": striped(np.random.permutation(T)[:S]),
        "n1": striped(np.random.permutation(S)[:W]),
        "n2": striped(np.random.permutation(S)[:W]),
        "n3": striped(np.random.randint(0, S, J)),
        "cand": striped(np.random.permutation(T)[:C]),
        "n4": striped8(np.stack([np.random.permutation(S) for _ in range(8)])),
        "n5": striped8(np.stack([np.random.permutation(S) for _ in range(8)])),
    }


def reference(x_words, x_scales, w1, gn, w2, gs, offs, n1, n2, n3, cand, n4, n5):
    xq = unpack_weight(x_words, x_scales)[:, unstriped(offs)]
    y = mxq(f64(w1), 0, "e4m3").T @ xq
    pa = y[:, unstriped(n2)]
    old = y[:, unstriped(n1)]
    ra = np.maximum(pa, 0.5 * old)
    ds = y.copy()
    ds[:, unstriped(n1)] = ra
    z = f64(gn) * ds
    a = mxq(f64(w2), 0, "e4m3").T @ mxq(z, 0, "e4m3")
    x_cand = unpack_weight(x_words, x_scales)[:, unstriped(cand)]
    mb = y[:, unstriped(n3)]
    ms = mb.reshape(H, S, 2).sum(axis=2)
    mx = mb.reshape(H, S, 2).max(axis=2)
    z2 = f64(gs) * (ms - np.maximum(y, mx))
    b = 0.0625 * ((x_cand.T @ mxq(z2, 0, "e4m3")))
    return np.maximum(a, b[np.arange(C)[:, None], runs(n5, C)]) - (np.minimum(a[np.arange(N)[:, None], runs(n4, N)], b))

from contextlib import ExitStack

import concourse.mybir as mybir

K, T, S, N, H, W, J, C = 512, 2048, 256, 512, 512, 192, 512, 512
FLOPS = 2 * S * (K * H + H * N + K * C)

F32 = mybir.dt.float32
BF16 = mybir.dt.bfloat16
I32 = mybir.dt.int32
U32 = mybir.dt.uint32
U16 = mybir.dt.uint16
U8 = mybir.dt.uint8
FP8X4 = mybir.dt.float8_e4m3fn_x4
ALU = mybir.AluOpType
COPY = mybir.ActivationFunctionType.Copy

P = 128
PACK = 4
Y_WINDOW = J + 32
AB_WINDOW = 2 * S


def tile_picked_fkcdmaxbkmaxgpair_none_p_kernel(
    tc, x_words, x_scales, w1, gn, w2, gs, offs, n1, n2, n3, cand, n4, n5, out
):
    nc = tc.nc
    tiles = range(PACK)

    with ExitStack() as ctx:
        sb = ctx.enter_context(tc.tile_pool(name="sb", bufs=1))
        psum = ctx.enter_context(tc.psum_pool(name="psum", bufs=1))

        def tile(name, shape, dtype):
            return sb.tile(shape, dtype, name=name, align_bytes=64)

        def load_list(name, src):
            dst = tile(name, list(src.shape), U16)
            nc.sync.dma_start(dst[:], src)
            return dst

        def load_weight(name, src):
            dst = tile(name, [P, PACK, src.shape[1]], F32)
            nc.sync.dma_start(dst[:], src.rearrange("(p j) c -> p j c", j=PACK))
            return dst

        def load_factor(name, src):
            dst = tile(name, [P, PACK], F32)
            nc.sync.dma_start(dst[:], src.rearrange("(p t) o -> p (t o)", t=PACK))
            return dst

        x_s = tile("x_s", [P, T], U8)
        nc.vector.memset(x_s[:].bitcast(I32), 0)
        offs_sb = load_list("offs_sb", offs)
        w1_raw = load_weight("w1_raw", w1)
        scale_rows = x_scales[0].rearrange("(q r) n -> r q n", r=4)
        for r in range(4):
            nc.sync.dma_start(x_s[r:P:32, :].bitcast(I32), scale_rows[r].bitcast(I32))
        x_w = tile("x_w", [P, T], I32)
        nc.sync.dma_start(x_w[:], x_words[0].rearrange("p n r -> p (n r)").bitcast(I32))
        cand_sb = load_list("cand_sb", cand)
        n3_sb = load_list("n3_sb", n3)
        gs_sb = load_factor("gs_sb", gs)
        w2_raw = load_weight("w2_raw", w2)
        n2_sb = load_list("n2_sb", n2)
        n1_sb = load_list("n1_sb", n1)
        gn_sb = load_factor("gn_sb", gn)
        n5_sb = load_list("n5_sb", n5)
        n4_sb = load_list("n4_sb", n4)

        y_win = [tile(f"y_win{t}", [P, Y_WINDOW], F32) for t in tiles]
        a_win = [tile(f"a_win{t}", [P, AB_WINDOW], F32) for t in tiles]
        b_win = [tile(f"b_win{t}", [P, AB_WINDOW], F32) for t in tiles]
        for win in y_win + b_win + a_win:
            nc.vector.memset(win[:, S:], 0.0)

        xq_s = tile("xq_s", [P, S], U8)
        nc.vector.tensor_copy(xq_s[:], x_s[:].indirect(offs_sb[:]))
        xc_s = tile("xc_s", [P, C], U8)
        nc.vector.tensor_copy(xc_s[:], x_s[:].indirect(cand_sb[:]))

        def round_pair(name, raw, half, on_scalar):
            grouped = tile(name, [P, 2, P, PACK], BF16)
            src = raw[:].rearrange("p j (m t) -> p m j t", t=PACK)[:, :, :, 2 * half : 2 * half + 2]
            dst = grouped[:].rearrange("p t m j -> p m j t")
            if on_scalar:
                nc.scalar.activation(dst, src, COPY)
            else:
                nc.vector.tensor_copy(dst, src)
            return grouped

        def quantize(name, grouped_flat):
            width = grouped_flat.shape[1] // PACK
            codes = tile(name + "_c", [P, width], U32)
            scales = tile(name + "_s", [P, width], U8)
            nc.vector.quantize_mx(out=codes[:].bitcast(FP8X4), scales=scales[:], in_=grouped_flat)
            return codes, scales

        def product(acc, stationary, t, moving):
            cols = slice(P * t, P * (t + 1))
            nc.tensor.matmul_mx(
                out=acc[:],
                lhsT=stationary[0][:, cols].bitcast(FP8X4),
                lhsT_scale=stationary[1][:, cols],
                rhs=moving[0][:].bitcast(FP8X4),
                rhs_scale=moving[1][:],
                start=True,
                stop=True,
            )

        w1_g = [round_pair(f"w1_g{h}", w1_raw, h, h == 1) for h in range(2)]
        w1_q = [quantize(f"w1_q{h}", w1_g[h][:].rearrange("p t m j -> p (t m j)")) for h in range(2)]

        xq_w = tile("xq_w", [P, S], U32)
        nc.vector.tensor_copy(xq_w[:], x_w[:].bitcast(U32).indirect(offs_sb[:]))

        y_ps = [psum.tile([P, S], F32, name=f"yb_ps{t}") for t in tiles]
        for t in tiles:
            product(y_ps[t], w1_q[t // 2], t % 2, (xq_w, xq_s))
            nc.vector.tensor_copy(y_win[t][:, :S], y_ps[t][:])

        mb = [tile(f"mb{t}", [P, J], F32) for t in tiles]
        for t in tiles:
            nc.scalar.activation(mb[t][:], y_win[t][:].indirect(n3_sb[:]), COPY)

        pa = [tile(f"pa{t}", [P, W], F32) for t in tiles]
        old = [tile(f"old{t}", [P, W], F32) for t in tiles]
        for t in tiles:
            nc.scalar.activation(pa[t][:], y_win[t][:].indirect(n2_sb[:]), COPY)
            nc.scalar.activation(old[t][:], y_win[t][:].indirect(n1_sb[:]), COPY)

        xc_w = tile("xc_w", [P, C], U32)
        nc.vector.tensor_copy(xc_w[:], x_w[:].bitcast(U32).indirect(cand_sb[:]))

        z2_g = tile("z2_g", [P, S, PACK], BF16)
        gap = [tile(f"gap{t}", [P, S], F32) for t in tiles]
        low = [tile(f"low{t}", [P, S], F32) for t in tiles]
        dif = [tile(f"dif{t}", [P, S], F32) for t in tiles]
        for pair in range(2):
            both = (2 * pair, 2 * pair + 1)
            for t in both:
                nc.vector.tensor_tensor(gap[t][:], mb[t][:, 0:J:2], y_ps[t][:], ALU.subtract)
            for t in both:
                nc.vector.scalar_tensor_tensor(low[t][:], gap[t][:], 0.0, mb[t][:, 1:J:2], ALU.min, ALU.add)
            for t in both:
                nc.vector.tensor_tensor(dif[t][:], low[t][:], mb[t][:, 0:J:2], ALU.min)
            for t in both:
                nc.vector.tensor_scalar(z2_g[:, :, t], dif[t][:], gs_sb[:, t : t + 1], None, ALU.mult)

        ra = [tile(f"ra{t}", [P, W], F32) for t in tiles]
        for t in tiles:
            nc.vector.scalar_tensor_tensor(ra[t][:], old[t][:], 0.5, pa[t][:], ALU.mult, ALU.max)
            nc.scalar.activation(y_win[t][:].indirect(n1_sb[:]), ra[t][:], COPY)

        z2_q = quantize("z2_q", z2_g[:].rearrange("p s t -> p (s t)"))
        xc_wd = tile("xc_wd", [P, C], U32)
        nc.vector.tensor_copy(
            xc_wd[:].rearrange("p (t m) -> p m t", t=PACK), xc_w[:].rearrange("p (m t) -> p m t", t=PACK)
        )
        xc_sd = tile("xc_sd", [P, C], U8)
        nc.vector.tensor_copy(
            xc_sd[:].rearrange("p (t m) -> p m t", t=PACK), xc_s[:].rearrange("p (m t) -> p m t", t=PACK)
        )
        b_ps = [psum.tile([P, S], F32, name=f"yb_ps{t}") for t in tiles]
        for t in tiles:
            product(b_ps[t], (xc_wd, xc_sd), t, z2_q)

        w2_g = [round_pair(f"w2_g{h}", w2_raw, h, False) for h in range(2)]
        w2_q = [quantize(f"w2_q{h}", w2_g[h][:].rearrange("p t m j -> p (t m j)")) for h in range(2)]

        for t in tiles:
            nc.vector.tensor_scalar(b_win[t][:, :S], b_ps[t][:], 0.0625, None, ALU.mult)

        z_g = tile("z_g", [P, S, PACK], BF16)
        for t in tiles:
            nc.vector.tensor_scalar(z_g[:, :, t], y_win[t][:, :S], gn_sb[:, t : t + 1], None, ALU.mult)
        z_q = quantize("z_q", z_g[:].rearrange("p s t -> p (s t)"))

        b5 = [tile(f"b5_{t}", [P, S], F32) for t in tiles]
        for t in tiles:
            nc.scalar.activation(b5[t][:], b_win[t][:].indirect(n5_sb[:]), COPY)

        a_ps = [psum.tile([P, S], F32, name=f"a_ps{t}") for t in tiles]
        for t in tiles:
            product(a_ps[t], w2_q[t // 2], t % 2, z_q)
            nc.vector.tensor_copy(a_win[t][:, :S], a_ps[t][:])

        a4 = [tile(f"a4_{t}", [P, S], F32) for t in tiles]
        for t in tiles:
            nc.scalar.activation(a4[t][:], a_win[t][:].indirect(n4_sb[:]), COPY)

        hi = [tile(f"hi{t}", [P, S], F32) for t in tiles]
        for t in tiles:
            nc.vector.tensor_tensor(hi[t][:], b5[t][:], a_ps[t][:], ALU.max)

        out_rows = out.rearrange("(p t) s -> p t s", t=PACK)
        for t in tiles:
            lo = tile(f"lo{t}", [P, S], F32)
            nc.vector.tensor_tensor(lo[:], a4[t][:], b_win[t][:, :S], ALU.min)
            res = tile(f"res{t}", [P, S], F32)
            nc.vector.tensor_tensor(res[:], hi[t][:], lo[:], ALU.subtract)
            nc.sync.dma_start(out_rows[:, t, :], res[:])
